import numpy as np
import ml_dtypes


def mxq(x, axis, fmt="e4m3"):
    dtype, down = {"e4m3": (ml_dtypes.float8_e4m3fn, 7), "e5m2": (ml_dtypes.float8_e5m2, 14)}[fmt]
    v = np.moveaxis(np.asarray(x, np.float32).astype(ml_dtypes.bfloat16).astype(np.float64), axis, -1)
    blocks = v.reshape(v.shape[:-1] + (-1, 32))
    amax = np.abs(blocks).max(-1, keepdims=True)
    byte = np.maximum(np.where(amax > 0, np.frexp(amax)[1] - 1 + 127, 0) - down, 1)
    scale = np.exp2(byte - 127.0)
    codes = (blocks / scale).astype(np.float32).astype(dtype).astype(np.float64)
    return np.moveaxis((codes * scale).reshape(v.shape), -1, axis)


WIDE = False


def mx_kscale(k, group=512):
    if not WIDE:
        return np.ones(k)
    levels = np.array([18, -18])
    if group != 512:
        return np.exp2(np.random.permutation(np.resize(levels, k // group))).repeat(group)
    if k % 512:
        return np.exp2(np.random.permutation(np.resize(levels, k // 32))).repeat(32)
    a = np.empty((k // 512, 16))
    for p in range(k // 512):
        a[p, :8] = np.random.permutation(np.resize(levels, 8))
        for g in range(8):
            far = levels[np.abs(levels - a[p, g]) >= 10]
            a[p, g + 8] = far[np.random.randint(len(far))]
    return np.exp2(a.ravel()).repeat(32)


def f64(x):
    return np.asarray(x).astype(np.float64)


G, D, M, N = 4, 128, 128, 512


def setup_inputs():
    n = np.random.standard_normal
    s_d = mx_kscale(D, 0)
    return {
        "x": (n((G, D, N)) * s_d[:, None]).astype(np.float32),
        "w": (np.where(np.arange(D)[:, None] <= np.arange(M)[None], 0.97 ** (np.arange(M)[None] - np.arange(D)[:, None]), 0.0) * 0.2 / s_d[:, None]).astype(np.float32),
        "dd": (np.random.uniform(0.5, 2.0, (1, N))).astype(np.float32),
        "xs": (n((G, M, N))).astype(np.float32),
        "x1": (n((G, M, N))).astype(np.float32),
    }


def reference(x, w, dd, xs, x1):
    wq = mxq(f64(w), 0, "e4m3")
    xq = mxq(f64(x), 1, "e4m3")
    z = wq.T @ xq
    y = (z + f64(dd) * f64(xs)) * f64(x1)
    return y

@@ -1,0 +1,126 @@
+from contextlib import ExitStack
+
+import concourse.mybir as mybir
+
+G, D, M, N = 4, 128, 128, 512
+FLOPS = 2 * G * D * M * N
+
+F32 = mybir.dt.float32
+BF16 = mybir.dt.bfloat16
+U32 = mybir.dt.uint32
+U8 = mybir.dt.uint8
+FP8X4 = mybir.dt.float8_e4m3fn_x4
+MULT = mybir.AluOpType.mult
+ADD = mybir.AluOpType.add
+
+P = 128
+PACK = 4
+ROWS = D // PACK
+SQ = 32
+HALF = N // 2
+
+
+def interleave_views(dst, src, lo, hi):
+    d = dst[:, lo:hi, :].rearrange("p (c i) t -> p c t i", i=4)
+    s = src[:, :, lo:hi].rearrange("p t (c i) -> p c t i", i=4)
+    return d, s
+
+
+def tile_rows_mix_hyena_kernel(tc, x, w, dd, xs, x1, out):
+    nc = tc.nc
+    with ExitStack() as ctx:
+        sb = ctx.enter_context(tc.tile_pool(name="sb", bufs=1))
+        ps = ctx.enter_context(tc.psum_pool(name="ps", bufs=1))
+        ctx.enter_context(tc.manual_schedule())
+
+        dd_rows = sb.tile([P, SQ], F32, align_bytes=64)
+        nc.sync.dma_start(
+            out=dd_rows[:],
+            in_=dd.rearrange("o (c j) -> o c j", j=SQ).broadcast_to([P * SQ // N, N // SQ, SQ]),
+        )
+        x_raw = sb.tile([P, PACK, N], F32)
+        nc.sync.dma_start(out=x_raw[:], in_=x.rearrange("g (p j) n -> (g p) j n", j=PACK))
+        w_raw = sb.tile([P, PACK, M], F32)
+        for g in range(G):
+            nc.sync.dma_start(out=w_raw[ROWS * g : ROWS * (g + 1)], in_=w.rearrange("(p j) m -> p j m", j=PACK))
+
+        xs_sb = [sb.tile([P, N], F32, name=f"xs{g}") for g in range(G)]
+        x1_sb = [sb.tile([P, N], F32, name=f"x1{g}") for g in range(G)]
+        nc.sync.dma_start(out=xs_sb[0][:], in_=xs[0])
+        for g in range(G):
+            if g + 1 < G:
+                nc.sync.dma_start(out=xs_sb[g + 1][:], in_=xs[g + 1])
+            nc.sync.dma_start(out=x1_sb[g][:], in_=x1[g])
+
+        dd_cols = sb.tile([P, SQ], F32, align_bytes=64)
+        nc.vector.transpose(out=dd_cols[:], in_=dd_rows[:])
+        dd_rep = sb.tile([P, N // SQ, SQ], F32, align_bytes=64)
+        nc.vector.tensor_copy(
+            out=dd_rep[:], in_=dd_cols[:, 0 : N // SQ].unsqueeze(2).to_broadcast([P, N // SQ, SQ])
+        )
+        dd_all = sb.tile([P, N], F32, align_bytes=64)
+        nc.vector.transpose(out=dd_all[:], in_=dd_rep[:].rearrange("p c i -> p (c i)"))
+
+        x_bf = [sb.tile([P, HALF, PACK], BF16, align_bytes=64, name=f"xbf{h}") for h in range(2)]
+        w_bf = sb.tile([P, M, PACK], BF16, align_bytes=64)
+        x_codes = sb.tile([P, N], U32, align_bytes=64)
+        x_scales = sb.tile([P, N], U8, align_bytes=64)
+        w_codes = sb.tile([P, M], U32, align_bytes=64)
+        w_scales = sb.tile([P, M], U8, align_bytes=64)
+
+        def cast_views(dst, src):
+            return dst.rearrange("p (c i) t -> p c t i", i=4), src.rearrange("p t (c i) -> p c t i", i=4)
+
+        d0, s0 = cast_views(x_bf[0][:], x_raw[:, :, 0:HALF])
+        nc.vector.tensor_copy(out=d0, in_=s0)
+        d1, s1 = cast_views(x_bf[1][:], x_raw[:, :, HALF:N])
+        nc.scalar.copy(out=d1, in_=s1)
+        dw, sw = cast_views(w_bf[:], w_raw[:])
+        nc.vector.tensor_copy(out=dw, in_=sw)
+
+        def quantize(codes, scales, src):
+            nc.vector.quantize_mx(out=codes.bitcast(FP8X4), scales=scales, in_=src.rearrange("p c t -> p (c t)"))
+
+        quantize(x_codes[:, 0:HALF], x_scales[:, 0:HALF], x_bf[0][:])
+        quantize(w_codes[:], w_scales[:], w_bf[:])
+        quantize(x_codes[:, HALF:N], x_scales[:, HALF:N], x_bf[1][:])
+
+        z = [ps.tile([M, N], F32, name=f"z{g}") for g in range(G)]
+        for g in range(G):
+            r = slice(ROWS * g, ROWS * (g + 1))
+            nc.tensor.matmul_mx(
+                out=z[g][:],
+                lhsT=w_codes[r, :].bitcast(FP8X4),
+                lhsT_scale=w_scales[r, :],
+                rhs=x_codes[r, :].bitcast(FP8X4),
+                rhs_scale=x_scales[r, :],
+                start=True,
+                stop=True,
+            )
+
+        t = [sb.tile([P, N], F32, name=f"t{g}") for g in range(G)]
+        u = [sb.tile([P, N], F32, name=f"u{g}") for g in range(G)]
+        y = [sb.tile([P, N], F32, name=f"y{g}") for g in range(G)]
+
+        def direct(g):
+            nc.vector.tensor_tensor(out=t[g][:], in0=xs_sb[g][:], in1=dd_all[:], op=MULT)
+
+        def total(g):
+            nc.vector.tensor_tensor(out=u[g][:], in0=z[g][:], in1=t[g][:], op=ADD)
+
+        def gate(g):
+            nc.vector.tensor_tensor(out=y[g][:], in0=u[g][:], in1=x1_sb[g][:], op=MULT)
+            nc.sync.dma_start(out=out[g], in_=y[g][:])
+
+        direct(0)
+        direct(1)
+        total(0)
+        total(1)
+        gate(0)
+        direct(2)
+        gate(1)
+        direct(3)
+        total(2)
+        total(3)
+        gate(2)
+        gate(3)

@@ -7,6 +7,7 @@ FLOPS = 2 * G * D * M * N
 
 F32 = mybir.dt.float32
 BF16 = mybir.dt.bfloat16
+I32 = mybir.dt.int32
 U32 = mybir.dt.uint32
 U8 = mybir.dt.uint8
 FP8X4 = mybir.dt.float8_e4m3fn_x4
@@ -20,12 +21,6 @@ SQ = 32
 HALF = N // 2
 
 
-def interleave_views(dst, src, lo, hi):
-    d = dst[:, lo:hi, :].rearrange("p (c i) t -> p c t i", i=4)
-    s = src[:, :, lo:hi].rearrange("p t (c i) -> p c t i", i=4)
-    return d, s
-
-
 def tile_rows_mix_hyena_kernel(tc, x, w, dd, xs, x1, out):
     nc = tc.nc
     with ExitStack() as ctx:
@@ -33,24 +28,33 @@ def tile_rows_mix_hyena_kernel(tc, x, w, dd, xs, x1, out):
         ps = ctx.enter_context(tc.psum_pool(name="ps", bufs=1))
         ctx.enter_context(tc.manual_schedule())
 
+        def cast_views(dst, src):
+            return dst.rearrange("p (c i) t -> p c t i", i=4), src.rearrange("p t (c i) -> p c t i", i=4)
+
+        def quantize(codes, scales, src):
+            nc.vector.quantize_mx(out=codes.bitcast(FP8X4), scales=scales, in_=src.rearrange("p c t -> p (c t)"))
+
+        w_q = sb.tile([P, M + M // 4], I32, align_bytes=64)
+        nc.gpsimd.memset(w_q[:, M:], 0)
+        w_codes = w_q[:, 0:M]
+        w_scales = w_q[:, M:].bitcast(U8)
+
         dd_rows = sb.tile([P, SQ], F32, align_bytes=64)
+        w_raw = sb.tile([ROWS, PACK, M], F32)
+        x_raw = sb.tile([P, PACK, N], F32)
+        xs_sb = [sb.tile([P, N], F32, name=f"xs{g}") for g in range(G)]
+        x1_sb = [sb.tile([P, N], F32, name=f"x1{g}") for g in range(G)]
         nc.sync.dma_start(
             out=dd_rows[:],
             in_=dd.rearrange("o (c j) -> o c j", j=SQ).broadcast_to([P * SQ // N, N // SQ, SQ]),
         )
-        x_raw = sb.tile([P, PACK, N], F32)
+        nc.sync.dma_start(out=w_raw[:], in_=w.rearrange("(p j) m -> p j m", j=PACK))
         nc.sync.dma_start(out=x_raw[:], in_=x.rearrange("g (p j) n -> (g p) j n", j=PACK))
-        w_raw = sb.tile([P, PACK, M], F32)
-        for g in range(G):
-            nc.sync.dma_start(out=w_raw[ROWS * g : ROWS * (g + 1)], in_=w.rearrange("(p j) m -> p j m", j=PACK))
-
-        xs_sb = [sb.tile([P, N], F32, name=f"xs{g}") for g in range(G)]
-        x1_sb = [sb.tile([P, N], F32, name=f"x1{g}") for g in range(G)]
         nc.sync.dma_start(out=xs_sb[0][:], in_=xs[0])
-        for g in range(G):
-            if g + 1 < G:
-                nc.sync.dma_start(out=xs_sb[g + 1][:], in_=xs[g + 1])
-            nc.sync.dma_start(out=x1_sb[g][:], in_=x1[g])
+
+        w_bf = sb.tile([ROWS, M, PACK], BF16, align_bytes=64)
+        dw, sw = cast_views(w_bf[:], w_raw[:])
+        nc.scalar.copy(out=dw, in_=sw)
 
         dd_cols = sb.tile([P, SQ], F32, align_bytes=64)
         nc.vector.transpose(out=dd_cols[:], in_=dd_rows[:])
@@ -58,69 +62,69 @@ def tile_rows_mix_hyena_kernel(tc, x, w, dd, xs, x1, out):
         nc.vector.tensor_copy(
             out=dd_rep[:], in_=dd_cols[:, 0 : N // SQ].unsqueeze(2).to_broadcast([P, N // SQ, SQ])
         )
+        quantize(w_codes[0:ROWS, :], w_scales[0:ROWS, :], w_bf[:])
         dd_all = sb.tile([P, N], F32, align_bytes=64)
         nc.vector.transpose(out=dd_all[:], in_=dd_rep[:].rearrange("p c i -> p (c i)"))
+        for g in range(1, G):
+            nc.sync.dma_start(out=w_q[ROWS * g : ROWS * (g + 1), :], in_=w_q[0:ROWS, :])
+
+        nc.sync.dma_start(out=xs_sb[1][:], in_=xs[1])
+        nc.sync.dma_start(out=xs_sb[2][:], in_=xs[2])
+        nc.sync.dma_start(out=x1_sb[0][:], in_=x1[0])
+        nc.sync.dma_start(out=xs_sb[3][:], in_=xs[3])
+        for g in range(1, G):
+            nc.sync.dma_start(out=x1_sb[g][:], in_=x1[g])
 
         x_bf = [sb.tile([P, HALF, PACK], BF16, align_bytes=64, name=f"xbf{h}") for h in range(2)]
-        w_bf = sb.tile([P, M, PACK], BF16, align_bytes=64)
         x_codes = sb.tile([P, N], U32, align_bytes=64)
         x_scales = sb.tile([P, N], U8, align_bytes=64)
-        w_codes = sb.tile([P, M], U32, align_bytes=64)
-        w_scales = sb.tile([P, M], U8, align_bytes=64)
-
-        def cast_views(dst, src):
-            return dst.rearrange("p (c i) t -> p c t i", i=4), src.rearrange("p t (c i) -> p c t i", i=4)
 
         d0, s0 = cast_views(x_bf[0][:], x_raw[:, :, 0:HALF])
         nc.vector.tensor_copy(out=d0, in_=s0)
         d1, s1 = cast_views(x_bf[1][:], x_raw[:, :, HALF:N])
         nc.scalar.copy(out=d1, in_=s1)
-        dw, sw = cast_views(w_bf[:], w_raw[:])
-        nc.vector.tensor_copy(out=dw, in_=sw)
-
-        def quantize(codes, scales, src):
-            nc.vector.quantize_mx(out=codes.bitcast(FP8X4), scales=scales, in_=src.rearrange("p c t -> p (c t)"))
-
-        quantize(x_codes[:, 0:HALF], x_scales[:, 0:HALF], x_bf[0][:])
-        quantize(w_codes[:], w_scales[:], w_bf[:])
-        quantize(x_codes[:, HALF:N], x_scales[:, HALF:N], x_bf[1][:])
 
         z = [ps.tile([M, N], F32, name=f"z{g}") for g in range(G)]
-        for g in range(G):
-            r = slice(ROWS * g, ROWS * (g + 1))
-            nc.tensor.matmul_mx(
-                out=z[g][:],
-                lhsT=w_codes[r, :].bitcast(FP8X4),
-                lhsT_scale=w_scales[r, :],
-                rhs=x_codes[r, :].bitcast(FP8X4),
-                rhs_scale=x_scales[r, :],
-                start=True,
-                stop=True,
-            )
-
         t = [sb.tile([P, N], F32, name=f"t{g}") for g in range(G)]
         u = [sb.tile([P, N], F32, name=f"u{g}") for g in range(G)]
         y = [sb.tile([P, N], F32, name=f"y{g}") for g in range(G)]
 
-        def direct(g):
-            nc.vector.tensor_tensor(out=t[g][:], in0=xs_sb[g][:], in1=dd_all[:], op=MULT)
+        def direct(g, eng=nc.vector):
+            eng.tensor_tensor(out=t[g][:], in0=xs_sb[g][:], in1=dd_all[:], op=MULT)
 
         def total(g):
             nc.vector.tensor_tensor(out=u[g][:], in0=z[g][:], in1=t[g][:], op=ADD)
 
-        def gate(g):
-            nc.vector.tensor_tensor(out=y[g][:], in0=u[g][:], in1=x1_sb[g][:], op=MULT)
-            nc.sync.dma_start(out=out[g], in_=y[g][:])
+        def gate(g, lo=0, hi=N, eng=nc.vector):
+            eng.tensor_tensor(out=y[g][:, lo:hi], in0=u[g][:, lo:hi], in1=x1_sb[g][:, lo:hi], op=MULT)
+            nc.sync.dma_start(out=out[g, :, lo:hi], in_=y[g][:, lo:hi])
+
+        def products():
+            for g in range(G):
+                r = slice(ROWS * g, ROWS * (g + 1))
+                nc.tensor.matmul_mx(
+                    out=z[g][:],
+                    lhsT=w_codes[r, :].bitcast(FP8X4),
+                    lhsT_scale=w_scales[r, :],
+                    rhs=x_codes[r, :].bitcast(FP8X4),
+                    rhs_scale=x_scales[r, :],
+                    start=True,
+                    stop=True,
+                )
 
         direct(0)
+        quantize(x_codes[:, 0:HALF], x_scales[:, 0:HALF], x_bf[0][:])
+        quantize(x_codes[:, HALF:N], x_scales[:, HALF:N], x_bf[1][:])
+        products()
         direct(1)
+        direct(2)
         total(0)
         total(1)
         gate(0)
-        direct(2)
-        gate(1)
         direct(3)
+        gate(1)
         total(2)
         total(3)
         gate(2)
-        gate(3)
+        gate(3, 0, HALF)
+        gate(3, HALF, N)

@@ -65,14 +65,12 @@ def tile_rows_mix_hyena_kernel(tc, x, w, dd, xs, x1, out):
         quantize(w_codes[0:ROWS, :], w_scales[0:ROWS, :], w_bf[:])
         dd_all = sb.tile([P, N], F32, align_bytes=64)
         nc.vector.transpose(out=dd_all[:], in_=dd_rep[:].rearrange("p c i -> p (c i)"))
-        for g in range(1, G):
-            nc.sync.dma_start(out=w_q[ROWS * g : ROWS * (g + 1), :], in_=w_q[0:ROWS, :])
-
         nc.sync.dma_start(out=xs_sb[1][:], in_=xs[1])
         nc.sync.dma_start(out=xs_sb[2][:], in_=xs[2])
-        nc.sync.dma_start(out=x1_sb[0][:], in_=x1[0])
-        nc.sync.dma_start(out=xs_sb[3][:], in_=xs[3])
         for g in range(1, G):
+            nc.sync.dma_start(out=w_q[ROWS * g : ROWS * (g + 1), :], in_=w_q[0:ROWS, :])
+        nc.sync.dma_start(out=xs_sb[3][:], in_=xs[3])
+        for g in range(G):
             nc.sync.dma_start(out=x1_sb[g][:], in_=x1[g])
 
         x_bf = [sb.tile([P, HALF, PACK], BF16, align_bytes=64, name=f"xbf{h}") for h in range(2)]
@@ -85,7 +83,7 @@ def tile_rows_mix_hyena_kernel(tc, x, w, dd, xs, x1, out):
         nc.scalar.copy(out=d1, in_=s1)
 
         z = [ps.tile([M, N], F32, name=f"z{g}") for g in range(G)]
-        t = [sb.tile([P, N], F32, name=f"t{g}") for g in range(G)]
+        t = [sb.tile([P, N], F32, name=f"t{g}") for g in range(G - 1)] + [xs_sb[1]]
         u = [sb.tile([P, N], F32, name=f"u{g}") for g in range(G)]
         y = [sb.tile([P, N], F32, name=f"y{g}") for g in range(G)]
 
@@ -97,6 +95,8 @@ def tile_rows_mix_hyena_kernel(tc, x, w, dd, xs, x1, out):
 
         def gate(g, lo=0, hi=N, eng=nc.vector):
             eng.tensor_tensor(out=y[g][:, lo:hi], in0=u[g][:, lo:hi], in1=x1_sb[g][:, lo:hi], op=MULT)
+
+        def store(g, lo=0, hi=N):
             nc.sync.dma_start(out=out[g, :, lo:hi], in_=y[g][:, lo:hi])
 
         def products():
@@ -118,13 +118,17 @@ def tile_rows_mix_hyena_kernel(tc, x, w, dd, xs, x1, out):
         products()
         direct(1)
         direct(2)
+        direct(3, nc.gpsimd)
         total(0)
+        gate(0, 0, 320, nc.gpsimd)
         total(1)
-        gate(0)
-        direct(3)
-        gate(1)
         total(2)
         total(3)
+        gate(0, 320, N)
+        store(0)
+        gate(1)
+        store(1)
         gate(2)
-        gate(3, 0, HALF)
-        gate(3, HALF, N)
+        store(2)
+        gate(3)
+        store(3)

@@ -19,6 +19,7 @@ PACK = 4
 ROWS = D // PACK
 SQ = 32
 HALF = N // 2
+N_MM = 128
 
 
 def tile_rows_mix_hyena_kernel(tc, x, w, dd, xs, x1, out):
@@ -28,11 +29,17 @@ def tile_rows_mix_hyena_kernel(tc, x, w, dd, xs, x1, out):
         ps = ctx.enter_context(tc.psum_pool(name="ps", bufs=1))
         ctx.enter_context(tc.manual_schedule())
 
+        def cols(h):
+            return slice(h * HALF, (h + 1) * HALF)
+
         def cast_views(dst, src):
             return dst.rearrange("p (c i) t -> p c t i", i=4), src.rearrange("p t (c i) -> p c t i", i=4)
 
         def quantize(codes, scales, src):
             nc.vector.quantize_mx(out=codes.bitcast(FP8X4), scales=scales, in_=src.rearrange("p c t -> p (c t)"))
+
+        def pair_rows(arr, h, q):
+            return arr[2 * q : 2 * q + 2, :, cols(h)].rearrange("g m n -> m g n")
 
         w_q = sb.tile([P, M + M // 4], I32, align_bytes=64)
         nc.gpsimd.memset(w_q[:, M:], 0)
@@ -41,94 +48,118 @@ def tile_rows_mix_hyena_kernel(tc, x, w, dd, xs, x1, out):
 
         dd_rows = sb.tile([P, SQ], F32, align_bytes=64)
         w_raw = sb.tile([ROWS, PACK, M], F32)
-        x_raw = sb.tile([P, PACK, N], F32)
-        xs_sb = [sb.tile([P, N], F32, name=f"xs{g}") for g in range(G)]
-        x1_sb = [sb.tile([P, N], F32, name=f"x1{g}") for g in range(G)]
+        x_rows = x.rearrange("g (p j) n -> (g p) j n", j=PACK)
+        x_raw = [sb.tile([P, PACK, HALF], F32, name=f"xraw{h}") for h in range(2)]
+        xs_sb = [[sb.tile([P, 2, HALF], F32, name=f"xs{h}{q}") for q in range(2)] for h in range(2)]
+        x1_sb = [[sb.tile([P, 2, HALF], F32, name=f"x1{h}{q}") for q in range(2)] for h in range(2)]
+
+        def load_x(h):
+            nc.sync.dma_start(out=x_raw[h][:], in_=x_rows[:, :, cols(h)])
+
+        def load_xs(h, q):
+            nc.sync.dma_start(out=xs_sb[h][q][:], in_=pair_rows(xs, h, q))
+
+        def load_x1(h, q):
+            nc.sync.dma_start(out=x1_sb[h][q][:], in_=pair_rows(x1, h, q))
+
+        nc.sync.dma_start(out=w_raw[:], in_=w.rearrange("(p j) m -> p j m", j=PACK))
         nc.sync.dma_start(
             out=dd_rows[:],
             in_=dd.rearrange("o (c j) -> o c j", j=SQ).broadcast_to([P * SQ // N, N // SQ, SQ]),
         )
-        nc.sync.dma_start(out=w_raw[:], in_=w.rearrange("(p j) m -> p j m", j=PACK))
-        nc.sync.dma_start(out=x_raw[:], in_=x.rearrange("g (p j) n -> (g p) j n", j=PACK))
-        nc.sync.dma_start(out=xs_sb[0][:], in_=xs[0])
+        load_x(0)
+        load_xs(0, 0)
+        load_xs(0, 1)
+        load_xs(1, 0)
 
         w_bf = sb.tile([ROWS, M, PACK], BF16, align_bytes=64)
         dw, sw = cast_views(w_bf[:], w_raw[:])
-        nc.scalar.copy(out=dw, in_=sw)
-
+        nc.vector.tensor_copy(out=dw, in_=sw)
         dd_cols = sb.tile([P, SQ], F32, align_bytes=64)
         nc.vector.transpose(out=dd_cols[:], in_=dd_rows[:])
-        dd_rep = sb.tile([P, N // SQ, SQ], F32, align_bytes=64)
-        nc.vector.tensor_copy(
-            out=dd_rep[:], in_=dd_cols[:, 0 : N // SQ].unsqueeze(2).to_broadcast([P, N // SQ, SQ])
-        )
         quantize(w_codes[0:ROWS, :], w_scales[0:ROWS, :], w_bf[:])
-        dd_all = sb.tile([P, N], F32, align_bytes=64)
-        nc.vector.transpose(out=dd_all[:], in_=dd_rep[:].rearrange("p c i -> p (c i)"))
-        nc.sync.dma_start(out=xs_sb[1][:], in_=xs[1])
-        nc.sync.dma_start(out=xs_sb[2][:], in_=xs[2])
+        blocks = HALF // SQ
+        dd_rep = [sb.tile([P, blocks, SQ], F32, align_bytes=64, name=f"ddrep{h}") for h in range(2)]
+        dd_all = [sb.tile([P, HALF], F32, align_bytes=64, name=f"ddall{h}") for h in range(2)]
+        for h in range(2):
+            nc.vector.tensor_copy(
+                out=dd_rep[h][:],
+                in_=dd_cols[:, h * blocks : (h + 1) * blocks].unsqueeze(2).to_broadcast([P, blocks, SQ]),
+            )
+        for h in range(2):
+            nc.vector.transpose(out=dd_all[h][:], in_=dd_rep[h][:].rearrange("p c i -> p (c i)"))
+
         for g in range(1, G):
             nc.sync.dma_start(out=w_q[ROWS * g : ROWS * (g + 1), :], in_=w_q[0:ROWS, :])
-        nc.sync.dma_start(out=xs_sb[3][:], in_=xs[3])
-        for g in range(G):
-            nc.sync.dma_start(out=x1_sb[g][:], in_=x1[g])
+        load_x(1)
+        load_x1(0, 0)
+        load_x1(0, 1)
+        load_xs(1, 1)
+        load_x1(1, 0)
+        load_x1(1, 1)
 
-        x_bf = [sb.tile([P, HALF, PACK], BF16, align_bytes=64, name=f"xbf{h}") for h in range(2)]
-        x_codes = sb.tile([P, N], U32, align_bytes=64)
-        x_scales = sb.tile([P, N], U8, align_bytes=64)
+        x_bf = [sb.tile([P, HALF, PACK], BF16, align_bytes=64, name=f"xbf{h}", tag=f"xbf{h}") for h in range(2)]
+        x_codes = [sb.tile([P, HALF], U32, align_bytes=64, name=f"xc{h}") for h in range(2)]
+        x_scales = [sb.tile([P, HALF], U8, align_bytes=64, name=f"xsc{h}") for h in range(2)]
+        for h in range(2):
+            dx, sx = cast_views(x_bf[h][:], x_raw[h][:])
+            nc.scalar.copy(out=dx, in_=sx)
 
-        d0, s0 = cast_views(x_bf[0][:], x_raw[:, :, 0:HALF])
-        nc.vector.tensor_copy(out=d0, in_=s0)
-        d1, s1 = cast_views(x_bf[1][:], x_raw[:, :, HALF:N])
-        nc.scalar.copy(out=d1, in_=s1)
+        z = [[ps.tile([M, HALF], F32, name=f"z{h}{g}") for g in range(G)] for h in range(2)]
+        t = {}
+        u = [[sb.tile([P, 2, HALF], F32, name=f"u{h}{q}") for q in range(2)] for h in range(2)]
+        y = [[sb.tile([P, 2, HALF], F32, name=f"y{h}{q}") for q in range(2)] for h in range(2)]
 
-        z = [ps.tile([M, N], F32, name=f"z{g}") for g in range(G)]
-        t = [sb.tile([P, N], F32, name=f"t{g}") for g in range(G - 1)] + [xs_sb[1]]
-        u = [sb.tile([P, N], F32, name=f"u{g}") for g in range(G)]
-        y = [sb.tile([P, N], F32, name=f"y{g}") for g in range(G)]
-
-        def direct(g, eng=nc.vector):
-            eng.tensor_tensor(out=t[g][:], in0=xs_sb[g][:], in1=dd_all[:], op=MULT)
-
-        def total(g):
-            nc.vector.tensor_tensor(out=u[g][:], in0=z[g][:], in1=t[g][:], op=ADD)
-
-        def gate(g, lo=0, hi=N, eng=nc.vector):
-            eng.tensor_tensor(out=y[g][:, lo:hi], in0=u[g][:, lo:hi], in1=x1_sb[g][:, lo:hi], op=MULT)
-
-        def store(g, lo=0, hi=N):
-            nc.sync.dma_start(out=out[g, :, lo:hi], in_=y[g][:, lo:hi])
-
-        def products():
+        def products(h):
+            quantize(x_codes[h][:], x_scales[h][:], x_bf[h][:])
             for g in range(G):
                 r = slice(ROWS * g, ROWS * (g + 1))
-                nc.tensor.matmul_mx(
-                    out=z[g][:],
-                    lhsT=w_codes[r, :].bitcast(FP8X4),
-                    lhsT_scale=w_scales[r, :],
-                    rhs=x_codes[r, :].bitcast(FP8X4),
-                    rhs_scale=x_scales[r, :],
-                    start=True,
-                    stop=True,
-                )
+                for c in range(0, HALF, N_MM):
+                    nc.tensor.matmul_mx(
+                        out=z[h][g][:, c : c + N_MM],
+                        lhsT=w_codes[r, :].bitcast(FP8X4),
+                        lhsT_scale=w_scales[r, :],
+                        rhs=x_codes[h][r, c : c + N_MM].bitcast(FP8X4),
+                        rhs_scale=x_scales[h][r, c : c + N_MM],
+                        start=True,
+                        stop=True,
+                    )
 
-        direct(0)
-        quantize(x_codes[:, 0:HALF], x_scales[:, 0:HALF], x_bf[0][:])
-        quantize(x_codes[:, HALF:N], x_scales[:, HALF:N], x_bf[1][:])
-        products()
-        direct(1)
-        direct(2)
-        direct(3, nc.gpsimd)
-        total(0)
-        gate(0, 0, 320, nc.gpsimd)
-        total(1)
-        total(2)
-        total(3)
-        gate(0, 320, N)
-        store(0)
-        gate(1)
-        store(1)
-        gate(2)
-        store(2)
-        gate(3)
-        store(3)
+        def direct(h, q, eng=nc.vector, tag=None):
+            t[h, q] = sb.tile([P, 2, HALF], F32, align_bytes=64, name=f"t{h}{q}", tag=tag or f"t{h}{q}")
+            eng.tensor_tensor(
+                out=t[h, q][:], in0=xs_sb[h][q][:], in1=dd_all[h][:].unsqueeze(1).to_broadcast([P, 2, HALF]), op=MULT
+            )
+
+        def total(h, g):
+            nc.vector.tensor_tensor(out=u[h][g // 2][:, g % 2, :], in0=z[h][g][:], in1=t[h, g // 2][:, g % 2, :], op=ADD)
+
+        def gate_pair(h, q):
+            nc.vector.tensor_tensor(out=y[h][q][:], in0=u[h][q][:], in1=x1_sb[h][q][:], op=MULT)
+            nc.sync.dma_start(out=pair_rows(out, h, q), in_=y[h][q][:])
+
+        def gate(h, g, eng=nc.vector):
+            q, e = divmod(g, 2)
+            eng.tensor_tensor(out=y[h][q][:, e, :], in0=u[h][q][:, e, :], in1=x1_sb[h][q][:, e, :], op=MULT)
+            nc.sync.dma_start(out=out[g, :, cols(h)], in_=y[h][q][:, e, :])
+
+        direct(0, 0)
+        products(0)
+        direct(1, 0, nc.gpsimd, "xbf0")
+        direct(0, 1)
+        total(0, 0)
+        total(0, 1)
+        total(0, 2)
+        total(0, 3)
+        gate_pair(0, 0)
+        products(1)
+        gate_pair(0, 1)
+        direct(1, 1)
+        total(1, 0)
+        gate(1, 0, nc.gpsimd)
+        total(1, 1)
+        total(1, 2)
+        total(1, 3)
+        gate(1, 1)
+        gate(1, 2)
+        gate(1, 3)

from contextlib import ExitStack

import concourse.mybir as mybir

G, D, M, N = 4, 128, 128, 512
FLOPS = 2 * G * D * M * N

F32 = mybir.dt.float32
BF16 = mybir.dt.bfloat16
I32 = mybir.dt.int32
U32 = mybir.dt.uint32
U8 = mybir.dt.uint8
FP8X4 = mybir.dt.float8_e4m3fn_x4
MULT = mybir.AluOpType.mult
ADD = mybir.AluOpType.add

P = 128
PACK = 4
ROWS = D // PACK
SQ = 32
HALF = N // 2
N_MM = 128


def tile_rows_mix_hyena_kernel(tc, x, w, dd, xs, x1, out):
    nc = tc.nc
    with ExitStack() as ctx:
        sb = ctx.enter_context(tc.tile_pool(name="sb", bufs=1))
        ps = ctx.enter_context(tc.psum_pool(name="ps", bufs=1))
        ctx.enter_context(tc.manual_schedule())

        def cols(h):
            return slice(h * HALF, (h + 1) * HALF)

        def cast_views(dst, src):
            return dst.rearrange("p (c i) t -> p c t i", i=4), src.rearrange("p t (c i) -> p c t i", i=4)

        def quantize(codes, scales, src):
            nc.vector.quantize_mx(out=codes.bitcast(FP8X4), scales=scales, in_=src.rearrange("p c t -> p (c t)"))

        def pair_rows(arr, h, q):
            return arr[2 * q : 2 * q + 2, :, cols(h)].rearrange("g m n -> m g n")

        w_q = sb.tile([P, M + M // 4], I32, align_bytes=64)
        nc.gpsimd.memset(w_q[:, M:], 0)
        w_codes = w_q[:, 0:M]
        w_scales = w_q[:, M:].bitcast(U8)

        dd_rows = sb.tile([P, SQ], F32, align_bytes=64)
        w_raw = sb.tile([ROWS, PACK, M], F32)
        x_rows = x.rearrange("g (p j) n -> (g p) j n", j=PACK)
        x_raw = [sb.tile([P, PACK, HALF], F32, name=f"xraw{h}") for h in range(2)]
        xs_sb = [[sb.tile([P, 2, HALF], F32, name=f"xs{h}{q}") for q in range(2)] for h in range(2)]
        x1_sb = [[sb.tile([P, 2, HALF], F32, name=f"x1{h}{q}") for q in range(2)] for h in range(2)]

        def load_x(h):
            nc.sync.dma_start(out=x_raw[h][:], in_=x_rows[:, :, cols(h)])

        def load_xs(h, q):
            nc.sync.dma_start(out=xs_sb[h][q][:], in_=pair_rows(xs, h, q))

        def load_x1(h, q):
            nc.sync.dma_start(out=x1_sb[h][q][:], in_=pair_rows(x1, h, q))

        nc.sync.dma_start(out=w_raw[:], in_=w.rearrange("(p j) m -> p j m", j=PACK))
        nc.sync.dma_start(
            out=dd_rows[:],
            in_=dd.rearrange("o (c j) -> o c j", j=SQ).broadcast_to([P * SQ // N, N // SQ, SQ]),
        )
        load_x(0)
        load_xs(0, 0)
        load_xs(0, 1)
        load_xs(1, 0)

        w_bf = sb.tile([ROWS, M, PACK], BF16, align_bytes=64)
        dw, sw = cast_views(w_bf[:], w_raw[:])
        nc.vector.tensor_copy(out=dw, in_=sw)
        dd_cols = sb.tile([P, SQ], F32, align_bytes=64)
        nc.vector.transpose(out=dd_cols[:], in_=dd_rows[:])
        quantize(w_codes[0:ROWS, :], w_scales[0:ROWS, :], w_bf[:])
        blocks = HALF // SQ
        dd_rep = [sb.tile([P, blocks, SQ], F32, align_bytes=64, name=f"ddrep{h}") for h in range(2)]
        dd_all = [sb.tile([P, HALF], F32, align_bytes=64, name=f"ddall{h}") for h in range(2)]
        for h in range(2):
            nc.vector.tensor_copy(
                out=dd_rep[h][:],
                in_=dd_cols[:, h * blocks : (h + 1) * blocks].unsqueeze(2).to_broadcast([P, blocks, SQ]),
            )
        for h in range(2):
            nc.vector.transpose(out=dd_all[h][:], in_=dd_rep[h][:].rearrange("p c i -> p (c i)"))

        for g in range(1, G):
            nc.sync.dma_start(out=w_q[ROWS * g : ROWS * (g + 1), :], in_=w_q[0:ROWS, :])
        load_x(1)
        load_x1(0, 0)
        load_x1(0, 1)
        load_xs(1, 1)
        load_x1(1, 0)
        load_x1(1, 1)

        x_bf = [sb.tile([P, HALF, PACK], BF16, align_bytes=64, name=f"xbf{h}", tag=f"xbf{h}") for h in range(2)]
        x_codes = [sb.tile([P, HALF], U32, align_bytes=64, name=f"xc{h}") for h in range(2)]
        x_scales = [sb.tile([P, HALF], U8, align_bytes=64, name=f"xsc{h}") for h in range(2)]
        for h in range(2):
            dx, sx = cast_views(x_bf[h][:], x_raw[h][:])
            nc.scalar.copy(out=dx, in_=sx)

        z = [[ps.tile([M, HALF], F32, name=f"z{h}{g}") for g in range(G)] for h in range(2)]
        t = {}
        u = [[sb.tile([P, 2, HALF], F32, name=f"u{h}{q}") for q in range(2)] for h in range(2)]
        y = [[sb.tile([P, 2, HALF], F32, name=f"y{h}{q}") for q in range(2)] for h in range(2)]

        def products(h):
            quantize(x_codes[h][:], x_scales[h][:], x_bf[h][:])
            for g in range(G):
                r = slice(ROWS * g, ROWS * (g + 1))
                for c in range(0, HALF, N_MM):
                    nc.tensor.matmul_mx(
                        out=z[h][g][:, c : c + N_MM],
                        lhsT=w_codes[r, :].bitcast(FP8X4),
                        lhsT_scale=w_scales[r, :],
                        rhs=x_codes[h][r, c : c + N_MM].bitcast(FP8X4),
                        rhs_scale=x_scales[h][r, c : c + N_MM],
                        start=True,
                        stop=True,
                    )

        def direct(h, q, eng=nc.vector, tag=None):
            t[h, q] = sb.tile([P, 2, HALF], F32, align_bytes=64, name=f"t{h}{q}", tag=tag or f"t{h}{q}")
            eng.tensor_tensor(
                out=t[h, q][:], in0=xs_sb[h][q][:], in1=dd_all[h][:].unsqueeze(1).to_broadcast([P, 2, HALF]), op=MULT
            )

        def total(h, g):
            nc.vector.tensor_tensor(out=u[h][g // 2][:, g % 2, :], in0=z[h][g][:], in1=t[h, g // 2][:, g % 2, :], op=ADD)

        def gate_pair(h, q):
            nc.vector.tensor_tensor(out=y[h][q][:], in0=u[h][q][:], in1=x1_sb[h][q][:], op=MULT)
            nc.sync.dma_start(out=pair_rows(out, h, q), in_=y[h][q][:])

        def gate(h, g, eng=nc.vector):
            q, e = divmod(g, 2)
            eng.tensor_tensor(out=y[h][q][:, e, :], in0=u[h][q][:, e, :], in1=x1_sb[h][q][:, e, :], op=MULT)
            nc.sync.dma_start(out=out[g, :, cols(h)], in_=y[h][q][:, e, :])

        direct(0, 0)
        products(0)
        direct(1, 0, nc.gpsimd, "xbf0")
        direct(0, 1)
        total(0, 0)
        total(0, 1)
        total(0, 2)
        total(0, 3)
        gate_pair(0, 0)
        products(1)
        gate_pair(0, 1)
        direct(1, 1)
        total(1, 0)
        gate(1, 0, nc.gpsimd)
        total(1, 1)
        total(1, 2)
        total(1, 3)
        gate(1, 1)
        gate(1, 2)
        gate(1, 3)
